import numpy as np
import ml_dtypes


def mxq(x, axis, fmt="e4m3"):
    dtype, down = {"e4m3": (ml_dtypes.float8_e4m3fn, 7), "e5m2": (ml_dtypes.float8_e5m2, 14)}[fmt]
    v = np.moveaxis(np.asarray(x, np.float32).astype(ml_dtypes.bfloat16).astype(np.float64), axis, -1)
    blocks = v.reshape(v.shape[:-1] + (-1, 32))
    amax = np.abs(blocks).max(-1, keepdims=True)
    byte = np.maximum(np.where(amax > 0, np.frexp(amax)[1] - 1 + 127, 0) - down, 1)
    scale = np.exp2(byte - 127.0)
    codes = (blocks / scale).astype(np.float32).astype(dtype).astype(np.float64)
    return np.moveaxis((codes * scale).reshape(v.shape), -1, axis)


WIDE = False


def mx_kscale(k):
    if not WIDE:
        return np.ones(k)
    levels = np.array([10, -10, 5, -5, 0])
    if k % 512:
        return np.exp2(np.random.permutation(np.resize(levels, k // 32))).repeat(32)
    a = np.empty((k // 512, 16))
    for p in range(k // 512):
        a[p, :8] = np.random.permutation(np.resize(levels, 8))
        for g in range(8):
            far = levels[np.abs(levels - a[p, g]) >= 10]
            a[p, g + 8] = far[np.random.randint(len(far))]
    return np.exp2(a.ravel()).repeat(32)


def f64(x):
    return np.asarray(x).astype(np.float64)


def striped(idx):
    return np.tile(idx.reshape(-1, 16).T, (8, 1)).astype(np.uint16)


def unstriped(offs):
    return offs[:16].T.reshape(-1).astype(np.int64)


def striped8(idx):
    return np.concatenate([x.reshape(-1, 16).T for x in idx]).astype(np.uint16)


def runs(offs, k):
    lists = np.stack([offs[16 * r : 16 * r + 16].T.reshape(-1) for r in range(8)]).astype(np.int64)
    return lists[np.arange(k) % 512 // 64]


def pack_weight(w):
    k, n = w.shape
    w = f64(np.asarray(w, np.float32).astype(ml_dtypes.bfloat16)).reshape(k // 32, 32, n)
    amax = np.abs(w).max(1)
    byte = np.clip(np.where(amax > 0, np.frexp(amax)[1] - 1 + 127 - 7, 1), 1, 254)
    scaled = (w * np.exp2(127.0 - byte)[:, None, :]).reshape(k, n).astype(np.float32)
    words = np.ascontiguousarray(scaled.reshape(k // 512, 128, 4, n).transpose(0, 1, 3, 2)).astype(ml_dtypes.float8_e4m3fn).view(np.uint8)
    return words, np.ascontiguousarray(byte.astype(np.uint8).reshape(k // 512, 16, n))


def unpack_weight(words, scales):
    g, p, n, _ = words.shape
    vals = np.ascontiguousarray(words).view(ml_dtypes.float8_e4m3fn).astype(np.float64) * np.repeat(np.exp2(scales.astype(np.float64) - 127.0), 8, axis=1)[..., None]
    return vals.transpose(0, 1, 3, 2).reshape(g * 512, n)


def sigmoid(v):
    return 1.0 / (1.0 + np.exp(-np.maximum(v, -700.0)))


K, T, S, N, H, W, C = 512, 2048, 512, 512, 512, 2048, 512


def setup_inputs():
    n = np.random.standard_normal
    s = mx_kscale(K)[:, None]
    u = mx_kscale(S)
    packed_xT = pack_weight(n((K, T)) * s)
    return {
        "x_words": packed_xT[0],
        "x_scales": packed_xT[1],
        "w1": (n((K, H)) / np.sqrt(K) / s).astype(np.float32),
        "w2": (n((K, H)) / np.sqrt(K) / s).astype(np.float32),
        "tau": np.random.uniform(0.3, 0.9, (H, 1)).astype(np.float32),
        "gn": (np.random.uniform(0.5, 1.5, (H, 1)) * u[:, None]).astype(np.float32),
        "w3": (n((H, N)) / np.sqrt(H) / u[:, None]).astype(np.float32),
        "gs": (np.random.uniform(0.5, 1.5, (K, 1)) / s).astype(np.float32),
        "sl": np.random.uniform(1.0, 2.0, (C, 1)).astype(np.float32),
        "th": (0.5 * n((C, 1))).astype(np.float32),
        "offs": striped(np.random.permutation(T)[:S]),
        "two": striped(np.random.permutation(T)[:S]),
        "n1": striped(np.random.randint(0, S, W)),
        "n2": striped(np.random.permutation(S)),
        "n3": striped(np.random.permutation(S)),
        "cand": striped(np.random.permutation(T)[:C]),
        "n4": striped8(np.stack([np.random.permutation(S) for _ in range(8)])),
        "n5": striped8(np.stack([np.random.permutation(S) for _ in range(8)])),
    }


def reference(x_words, x_scales, w1, w2, tau, gn, w3, gs, sl, th, offs, two, n1, n2, n3, cand, n4, n5):
    xq = unpack_weight(x_words, x_scales)[:, unstriped(offs)]
    y = mxq(f64(w1), 0, "e4m3").T @ xq
    mb = y[:, unstriped(n1)]
    mx = mb.reshape(H, S, 4).max(axis=2)
    mn = mb.reshape(H, S, 4).min(axis=2)
    z = f64(gn) * (mx - (0.5 * mn))
    a = mxq(f64(w3), 0, "e4m3").T @ mxq(z, 0, "e4m3")
    x_cand = unpack_weight(x_words, x_scales)[:, unstriped(cand)]
    x_two = unpack_weight(x_words, x_scales)[:, unstriped(two)]
    d = mxq(f64(w2), 0, "e4m3").T @ x_two
    top = d.max(axis=1, keepdims=True)
    ea = np.exp(f64(tau) * (d[:, unstriped(n2)] - top))
    z2 = f64(gs) * (np.maximum(d, 2.0 * ea) - (0.5 * d[:, unstriped(n3)]))
    b = 0.0625 * ((x_cand.T @ mxq(z2, 0, "e4m3")))
    sg = sigmoid(f64(sl) * (b[np.arange(C)[:, None], runs(n4, C)] - f64(th)))
    return np.maximum(a * sg, b[np.arange(C)[:, None], runs(n5, C)] - b)

@@ -1,0 +1,274 @@
+from contextlib import ExitStack
+
+import concourse.mybir as mybir
+
+F32 = mybir.dt.float32
+BF16 = mybir.dt.bfloat16
+I32 = mybir.dt.int32
+U32 = mybir.dt.uint32
+U16 = mybir.dt.uint16
+U8 = mybir.dt.uint8
+FP8X4 = mybir.dt.float8_e4m3fn_x4
+ALU = mybir.AluOpType
+ACT = mybir.ActivationFunctionType
+
+P = 128
+R = 4
+S = 512
+T = 2048
+WIDE = 1024
+NARROW = 544
+CHUNK = 128
+FLOPS = 4 * 2 * 512 * 512 * 512
+N3_FUSED = (0, 1, 2, 3)
+N5_FUSED = ()
+CAST = {"w1": "scalar", "w2": "scalar", "w3": "scalar"}
+
+
+def tile_picked_tfcdmxbgspanecl_none_p_kernel(
+    tc, x_words, x_scales, w1, w2, tau, gn, w3, gs, sl, th, offs, two, n1, n2, n3, cand, n4, n5, out
+):
+    nc = tc.nc
+    with ExitStack() as ctx:
+        keep = ctx.enter_context(tc.tile_pool(name="keep", bufs=1))
+        ring = ctx.enter_context(tc.tile_pool(name="ring", bufs=2))
+        psum = ctx.enter_context(tc.psum_pool(name="psum", bufs=1))
+
+        def sb(shape, dtype, name):
+            return keep.tile(shape, dtype, name=name, align_bytes=64)
+
+        def load_list(src, name):
+            tile = sb([P, src.shape[1]], U16, name)
+            nc.sync.dma_start(tile[:], src)
+            return tile
+
+        def load_rows(src, name):
+            tile = sb([P, R], F32, name)
+            nc.gpsimd.dma_start(tile[:], src.rearrange("(p t) one -> p (t one)", t=R))
+            return tile
+
+        def load_weight(src, name):
+            halves = []
+            for h in range(2):
+                raw = sb([P, R, S // 2], F32, "%s_raw%d" % (name, h))
+                nc.sync.dma_start(raw[:], src[:, h * (S // 2) : (h + 1) * (S // 2)].rearrange("(p j) c -> p j c", j=R))
+                halves.append(raw)
+            return halves
+
+        def round_weight(halves, name):
+            grouped = sb([P, R * S], BF16, name + "_bf16")
+            dealt = grouped[:].rearrange("p (t m j) -> p m j t", t=R, j=R)
+            for h, raw in enumerate(halves):
+                dst = dealt[:, h * (P // 2) : (h + 1) * (P // 2)]
+                src = raw[:].rearrange("p j (m t) -> p m j t", t=R)
+                if CAST[name] == "scalar":
+                    nc.scalar.copy(dst, src)
+                elif CAST[name] == "vector":
+                    nc.vector.tensor_copy(dst, src)
+                else:
+                    nc.gpsimd.tensor_scalar(dst, src, 1.0, 0.0, ALU.mult, ALU.add)
+            return grouped
+
+        def quantise(values, name):
+            codes = sb([P, S], U32, name + "_codes")
+            scales = sb([P, S], U8, name + "_scales")
+            nc.vector.quantize_mx(out=codes[:].bitcast(FP8X4), scales=scales[:], in_=values[:])
+            return codes, scales
+
+        def pick(lst, name, deal):
+            codes = sb([P, S], U32, name + "_codes")
+            scales = sb([P, S], U8, name + "_scales")
+            for dst, table in ((codes, xw), (scales, xs)):
+                view = dst[:].rearrange("p (t m) -> p m t", t=R) if deal else dst[:]
+                nc.vector.tensor_copy(view, table[:].indirect(lst[:]))
+            return codes, scales
+
+        def product(stationary, moving, t, bank):
+            acc = psum.tile([P, S], F32, name="bank%d" % bank)
+            cols = slice(t * P, (t + 1) * P)
+            nc.tensor.matmul_mx(
+                out=acc[:],
+                lhsT=stationary[0][:, cols].bitcast(FP8X4),
+                lhsT_scale=stationary[1][:, cols],
+                rhs=moving[0][:].bitcast(FP8X4),
+                rhs_scale=moving[1][:],
+                start=True,
+                stop=True,
+            )
+            return acc
+
+        xw = sb([P, T], U32, "xw")
+        xs = sb([P, T], U8, "xs")
+        nc.vector.memset(xs[:].bitcast(I32), 0)
+        xs_landing = sb([P, T], U8, "xs_landing")
+        for q in range(4):
+            nc.sync.dma_start(xs_landing[32 * q : 32 * q + 4, :].bitcast(I32), x_scales[0, 4 * q : 4 * q + 4, :].bitcast(I32))
+        two_t = load_list(two, "two_t")
+        nc.sync.dma_start(xw[:].bitcast(I32), x_words[0].rearrange("p n t -> p (n t)").bitcast(I32))
+        w2_raw = load_weight(w2, "w2")
+        offs_t = load_list(offs, "offs_t")
+        w1_raw = load_weight(w1, "w1")
+        cand_t = load_list(cand, "cand_t")
+        n2_t = load_list(n2, "n2_t")
+        n3_t = load_list(n3, "n3_t")
+        n1_t = load_list(n1, "n1_t")
+        w3_raw = load_weight(w3, "w3")
+        n4_t = load_list(n4, "n4_t")
+        n5_t = load_list(n5, "n5_t")
+        tau_t = load_rows(tau, "tau_t")
+        gs_t = load_rows(gs, "gs_t")
+        gn_t = load_rows(gn, "gn_t")
+        sl_t = load_rows(sl, "sl_t")
+        th_t = load_rows(th, "th_t")
+
+        wide = [sb([P, WIDE], F32, "wide%d" % t) for t in range(R)]
+        y_rows = [sb([P, NARROW], F32, "y_rows%d" % t) for t in range(R)]
+        half_d = {t: sb([P, NARROW], F32, "half_d%d" % t) for t in N3_FUSED}
+        for t in range(R):
+            nc.vector.memset(wide[t][:, S:], 0.0)
+        for tile in y_rows + list(half_d.values()):
+            nc.vector.memset(tile[:, S:], 0.0)
+
+        for q in range(4):
+            rows = slice(32 * q, 32 * q + 4)
+            nc.vector.tensor_copy(xs[rows, :].bitcast(I32), xs_landing[rows, :].bitcast(I32))
+        x_two = pick(two_t, "x_two", False)
+        x_idx = pick(offs_t, "x_idx", False)
+        neg_tau = sb([P, R], F32, "neg_tau")
+        nc.vector.tensor_scalar(neg_tau[:], tau_t[:], -1.0, None, ALU.mult)
+        w2_q = quantise(round_weight(w2_raw, "w2"), "w2")
+        w1_bf16 = round_weight(w1_raw, "w1")
+
+        top = sb([P, R], F32, "top")
+        exp_bias = sb([P, R], F32, "exp_bias")
+        ea = sb([P, R, S], F32, "ea")
+        for t in range(R):
+            col = slice(t, t + 1)
+            d_acc = product(w2_q, x_two, t, t)
+            nc.vector.tensor_scalar(wide[t][:, :S], d_acc[:], 1.0, None, ALU.mult, ALU.max, accum_out=top[:, col])
+            nc.scalar.activation(exp_bias[:, col], top[:, col], ACT.Copy, scale=neg_tau[:, col])
+            nc.scalar.activation(ea[:, t, :], wide[t][:].indirect(n2_t[:]), ACT.Exp, bias=exp_bias[:, col], scale=tau_t[:, col])
+            if t in N3_FUSED:
+                nc.scalar.activation(half_d[t][:, :S], d_acc[:], ACT.Copy, scale=-0.5)
+        w1_q = quantise(w1_bf16, "w1")
+        x_cand = pick(cand_t, "x_cand", True)
+
+        larger = sb([P, R, S], F32, "larger")
+        mixed = sb([P, R, S], F32, "mixed")
+        d_n3 = {t: sb([P, S], F32, "d_n3_%d" % t) for t in range(R) if t not in N3_FUSED}
+        for t in d_n3:
+            nc.scalar.activation(d_n3[t][:], wide[t][:].indirect(n3_t[:]), ACT.Copy)
+
+        def finish_mixed(t):
+            if t in N3_FUSED:
+                nc.vector.tensor_tensor(mixed[:, t, :], half_d[t][:].indirect(n3_t[:]), larger[:, t, :], ALU.add)
+            else:
+                nc.vector.scalar_tensor_tensor(mixed[:, t, :], d_n3[t][:], -0.5, larger[:, t, :], ALU.mult, ALU.add)
+
+        for t in range(R):
+            nc.vector.scalar_tensor_tensor(larger[:, t, :], ea[:, t, :], 2.0, wide[t][:, :S], ALU.mult, ALU.max)
+            if t > 0:
+                finish_mixed(t - 1)
+        finish_mixed(R - 1)
+
+        for t in range(R):
+            y_acc = product(w1_q, x_idx, t, R + t)
+            nc.scalar.copy(y_rows[t][:, :S], y_acc[:])
+
+        z2 = sb([P, S * R], BF16, "z2")
+        nc.vector.tensor_tensor(
+            z2[:].rearrange("p (c i t) -> p c t i", i=4, t=R),
+            mixed[:].rearrange("p t (c i) -> p c t i", i=4),
+            gs_t[:].unsqueeze(1).unsqueeze(3).to_broadcast([P, S // 4, R, 4]),
+            ALU.mult,
+        )
+        sig_bias = sb([P, R], F32, "sig_bias")
+        nc.vector.scalar_tensor_tensor(sig_bias[:], sl_t[:], -1.0, th_t[:], ALU.mult, ALU.mult)
+        z2_q = quantise(z2, "z2")
+        b_acc = [product(x_cand, z2_q, t, t) for t in range(R)]
+
+        z = sb([P, S * R], BF16, "z")
+        z_codes = sb([P, S], U32, "z_codes")
+        z_scales = sb([P, S], U8, "z_scales")
+        width = CHUNK * R
+        chunks = S // CHUNK
+        stage = {}
+
+        def fetch(c):
+            members = keep.tile([P, R, width], F32, name="members%d" % c)
+            for t in range(R):
+                nc.scalar.activation(members[:, t, :], y_rows[t][:].indirect(n1_t[:, c * width // 16 : (c + 1) * width // 16]), ACT.Copy)
+            stage[c, "members"] = members
+
+        def pairs(c, op, name):
+            view = stage[c, "members"][:].rearrange("p t (j h e) -> p h j t e", h=2, e=2)
+            tile = ring.tile([P, CHUNK, R, 2], F32, name=name)
+            nc.vector.tensor_tensor(tile[:], view[:, 0], view[:, 1], op)
+            stage[c, name] = tile
+
+        def fours(c, op, src, name):
+            view = stage[c, src][:].rearrange("p j t e -> p e (j t)")
+            tile = ring.tile([P, width], F32, name=name)
+            nc.vector.tensor_tensor(tile[:], view[:, 0], view[:, 1], op)
+            stage[c, name] = tile
+
+        def spread(c):
+            tile = ring.tile([P, width], F32, name="spread")
+            nc.vector.scalar_tensor_tensor(tile[:], stage[c, "mn"][:], -0.5, stage[c, "mx"][:], ALU.mult, ALU.add)
+            stage[c, "spread"] = tile
+
+        def gain(c):
+            nc.vector.tensor_tensor(
+                z[:, c * width : (c + 1) * width].rearrange("p (j t) -> p j t", t=R),
+                stage[c, "spread"][:].rearrange("p (j t) -> p j t", t=R),
+                gn_t[:].unsqueeze(1).to_broadcast([P, CHUNK, R]),
+                ALU.mult,
+            )
+
+        def quantise_chunk(c):
+            cols = slice(c * CHUNK, (c + 1) * CHUNK)
+            nc.vector.quantize_mx(out=z_codes[:, cols].bitcast(FP8X4), scales=z_scales[:, cols], in_=z[:, c * width : (c + 1) * width])
+
+        for c in range(chunks + 1):
+            if c < chunks:
+                fetch(c)
+                pairs(c, ALU.max, "hi")
+            if c > 0:
+                spread(c - 1)
+            if c < chunks:
+                pairs(c, ALU.min, "lo")
+            if c > 0:
+                gain(c - 1)
+            if c < chunks:
+                fours(c, ALU.max, "hi", "mx")
+            if c == chunks:
+                w3_q = quantise(round_weight(w3_raw, "w3"), "w3")
+            if c > 0:
+                quantise_chunk(c - 1)
+            if c < chunks:
+                fours(c, ALU.min, "lo", "mn")
+
+        b_again = {t: sb([P, S], F32, "b_again%d" % t) for t in N5_FUSED}
+        for t in range(R):
+            nc.scalar.activation(wide[t][:, :S], b_acc[t][:], ACT.Copy, scale=0.0625)
+            if t in N5_FUSED:
+                nc.sync.dma_start(b_again[t][:], wide[t][:, :S])
+
+        out_rows = out.rearrange("(p t) n -> p t n", t=R)
+        sg = sb([P, R, S], F32, "sg")
+        for t in range(R):
+            col = slice(t, t + 1)
+            step = sb([P, S], F32, "step%d" % t)
+            if t in N5_FUSED:
+                nc.vector.tensor_tensor(step[:], wide[t][:].indirect(n5_t[:]), b_again[t][:], ALU.subtract)
+            else:
+                b_n5 = sb([P, S], F32, "b_n5_%d" % t)
+                nc.scalar.activation(b_n5[:], wide[t][:].indirect(n5_t[:]), ACT.Copy)
+                nc.vector.tensor_tensor(step[:], b_n5[:], wide[t][:, :S], ALU.subtract)
+            nc.scalar.activation(sg[:, t, :], wide[t][:].indirect(n4_t[:]), ACT.Sigmoid, bias=sig_bias[:, col], scale=sl_t[:, col])
+            a_acc = product(w3_q, (z_codes, z_scales), t, R + t)
+            gated = sb([P, S], F32, "gated%d" % t)
+            nc.vector.tensor_tensor(gated[:], a_acc[:], sg[:, t, :], ALU.mult)
+            result = sb([P, S], F32, "result%d" % t)
+            nc.vector.tensor_tensor(result[:], gated[:], step[:], ALU.max)
+            nc.sync.dma_start(out_rows[:, t, :], result[:])

@@ -22,7 +22,7 @@ CHUNK = 128
 FLOPS = 4 * 2 * 512 * 512 * 512
 N3_FUSED = (0, 1, 2, 3)
 N5_FUSED = ()
-CAST = {"w1": "scalar", "w2": "scalar", "w3": "scalar"}
+CAST = {"w1": "scalar", "w2": "scalar", "w3": "vector"}
 
 
 def tile_picked_tfcdmxbgspanecl_none_p_kernel(
@@ -44,7 +44,7 @@ def tile_picked_tfcdmxbgspanecl_none_p_kernel(
 
         def load_rows(src, name):
             tile = sb([P, R], F32, name)
-            nc.gpsimd.dma_start(tile[:], src.rearrange("(p t) one -> p (t one)", t=R))
+            nc.sync.dma_start(tile[:], src.rearrange("(p t) one -> p (t one)", t=R))
             return tile
 
         def load_weight(src, name):
@@ -78,7 +78,7 @@ def tile_picked_tfcdmxbgspanecl_none_p_kernel(
         def pick(lst, name, deal):
             codes = sb([P, S], U32, name + "_codes")
             scales = sb([P, S], U8, name + "_scales")
-            for dst, table in ((codes, xw), (scales, xs)):
+            for dst, table in ((scales, xs), (codes, xw)):
                 view = dst[:].rearrange("p (t m) -> p m t", t=R) if deal else dst[:]
                 nc.vector.tensor_copy(view, table[:].indirect(lst[:]))
             return codes, scales
@@ -104,23 +104,26 @@ def tile_picked_tfcdmxbgspanecl_none_p_kernel(
         for q in range(4):
             nc.sync.dma_start(xs_landing[32 * q : 32 * q + 4, :].bitcast(I32), x_scales[0, 4 * q : 4 * q + 4, :].bitcast(I32))
         two_t = load_list(two, "two_t")
+        offs_t = load_list(offs, "offs_t")
         nc.sync.dma_start(xw[:].bitcast(I32), x_words[0].rearrange("p n t -> p (n t)").bitcast(I32))
         w2_raw = load_weight(w2, "w2")
-        offs_t = load_list(offs, "offs_t")
+        tau_t = load_rows(tau, "tau_t")
         w1_raw = load_weight(w1, "w1")
         cand_t = load_list(cand, "cand_t")
         n2_t = load_list(n2, "n2_t")
+        sl_t = load_rows(sl, "sl_t")
+        th_t = load_rows(th, "th_t")
+        gs_t = load_rows(gs, "gs_t")
         n3_t = load_list(n3, "n3_t")
         n1_t = load_list(n1, "n1_t")
+        gn_t = load_rows(gn, "gn_t")
         w3_raw = load_weight(w3, "w3")
         n4_t = load_list(n4, "n4_t")
         n5_t = load_list(n5, "n5_t")
-        tau_t = load_rows(tau, "tau_t")
-        gs_t = load_rows(gs, "gs_t")
-        gn_t = load_rows(gn, "gn_t")
-        sl_t = load_rows(sl, "sl_t")
-        th_t = load_rows(th, "th_t")
 
+        for q in range(4):
+            rows = slice(32 * q, 32 * q + 4)
+            nc.vector.tensor_copy(xs[rows, :].bitcast(I32), xs_landing[rows, :].bitcast(I32))
         wide = [sb([P, WIDE], F32, "wide%d" % t) for t in range(R)]
         y_rows = [sb([P, NARROW], F32, "y_rows%d" % t) for t in range(R)]
         half_d = {t: sb([P, NARROW], F32, "half_d%d" % t) for t in N3_FUSED}
@@ -129,9 +132,6 @@ def tile_picked_tfcdmxbgspanecl_none_p_kernel(
         for tile in y_rows + list(half_d.values()):
             nc.vector.memset(tile[:, S:], 0.0)
 
-        for q in range(4):
-            rows = slice(32 * q, 32 * q + 4)
-            nc.vector.tensor_copy(xs[rows, :].bitcast(I32), xs_landing[rows, :].bitcast(I32))
         x_two = pick(two_t, "x_two", False)
         x_idx = pick(offs_t, "x_idx", False)
         neg_tau = sb([P, R], F32, "neg_tau")
@@ -175,16 +175,21 @@ def tile_picked_tfcdmxbgspanecl_none_p_kernel(
             y_acc = product(w1_q, x_idx, t, R + t)
             nc.scalar.copy(y_rows[t][:, :S], y_acc[:])
 
-        z2 = sb([P, S * R], BF16, "z2")
-        nc.vector.tensor_tensor(
-            z2[:].rearrange("p (c i t) -> p c t i", i=4, t=R),
-            mixed[:].rearrange("p t (c i) -> p c t i", i=4),
-            gs_t[:].unsqueeze(1).unsqueeze(3).to_broadcast([P, S // 4, R, 4]),
-            ALU.mult,
-        )
         sig_bias = sb([P, R], F32, "sig_bias")
         nc.vector.scalar_tensor_tensor(sig_bias[:], sl_t[:], -1.0, th_t[:], ALU.mult, ALU.mult)
-        z2_q = quantise(z2, "z2")
+        z2 = sb([P, S * R], BF16, "z2")
+        z2_q = (sb([P, S], U32, "z2_codes"), sb([P, S], U8, "z2_scales"))
+        half = S // 2
+        for h in range(2):
+            nc.vector.tensor_tensor(
+                z2[:, h * half * R : (h + 1) * half * R].rearrange("p (c i t) -> p c t i", i=4, t=R),
+                mixed[:, :, h * half : (h + 1) * half].rearrange("p t (c i) -> p c t i", i=4),
+                gs_t[:].unsqueeze(1).unsqueeze(3).to_broadcast([P, half // 4, R, 4]),
+                ALU.mult,
+            )
+        for h in range(2):
+            cols = slice(h * half, (h + 1) * half)
+            nc.vector.quantize_mx(out=z2_q[0][:, cols].bitcast(FP8X4), scales=z2_q[1][:, cols], in_=z2[:, h * half * R : (h + 1) * half * R])
         b_acc = [product(x_cand, z2_q, t, t) for t in range(R)]
 
         z = sb([P, S * R], BF16, "z")
@@ -229,7 +234,26 @@ def tile_picked_tfcdmxbgspanecl_none_p_kernel(
             cols = slice(c * CHUNK, (c + 1) * CHUNK)
             nc.vector.quantize_mx(out=z_codes[:, cols].bitcast(FP8X4), scales=z_scales[:, cols], in_=z[:, c * width : (c + 1) * width])
 
+        b_again = {t: sb([P, S], F32, "b_again%d" % t) for t in N5_FUSED}
+        step = [sb([P, S], F32, "step%d" % t) for t in range(R)]
+
+        def empty_b():
+            for t in range(R):
+                nc.scalar.activation(wide[t][:, :S], b_acc[t][:], ACT.Copy, scale=0.0625)
+                if t in N5_FUSED:
+                    nc.sync.dma_start(b_again[t][:], wide[t][:, :S])
+
+        def fused_step(t):
+            nc.vector.tensor_tensor(step[t][:], wide[t][:].indirect(n5_t[:]), b_again[t][:], ALU.subtract)
+
         for c in range(chunks + 1):
+            if c == 4:
+                empty_b()
+            if c == 0:
+                w3_bf16 = round_weight(w3_raw, "w3")
+            if c == 4:
+                for t in N5_FUSED:
+                    fused_step(t)
             if c < chunks:
                 fetch(c)
                 pairs(c, ALU.max, "hi")
@@ -242,33 +266,38 @@ def tile_picked_tfcdmxbgspanecl_none_p_kernel(
             if c < chunks:
                 fours(c, ALU.max, "hi", "mx")
             if c == chunks:
-                w3_q = quantise(round_weight(w3_raw, "w3"), "w3")
+                w3_q = quantise(w3_bf16, "w3")
             if c > 0:
                 quantise_chunk(c - 1)
             if c < chunks:
                 fours(c, ALU.min, "lo", "mn")
 
-        b_again = {t: sb([P, S], F32, "b_again%d" % t) for t in N5_FUSED}
-        for t in range(R):
-            nc.scalar.activation(wide[t][:, :S], b_acc[t][:], ACT.Copy, scale=0.0625)
-            if t in N5_FUSED:
-                nc.sync.dma_start(b_again[t][:], wide[t][:, :S])
 
         out_rows = out.rearrange("(p t) n -> p t n", t=R)
-        sg = sb([P, R, S], F32, "sg")
+        sg = [sb([P, S], F32, "sg%d" % t) for t in range(R)]
+        gated = [sb([P, S], F32, "gated%d" % t) for t in range(R)]
+        result = [sb([P, S], F32, "result%d" % t) for t in range(R)]
+
+        def finish(t, cols):
+            nc.vector.tensor_tensor(result[t][:, cols], gated[t][:, cols], step[t][:, cols], ALU.max)
+            nc.sync.dma_start(out_rows[:, t, cols], result[t][:, cols])
+
         for t in range(R):
-            col = slice(t, t + 1)
-            step = sb([P, S], F32, "step%d" % t)
-            if t in N5_FUSED:
-                nc.vector.tensor_tensor(step[:], wide[t][:].indirect(n5_t[:]), b_again[t][:], ALU.subtract)
-            else:
+            if t not in N5_FUSED:
                 b_n5 = sb([P, S], F32, "b_n5_%d" % t)
                 nc.scalar.activation(b_n5[:], wide[t][:].indirect(n5_t[:]), ACT.Copy)
-                nc.vector.tensor_tensor(step[:], b_n5[:], wide[t][:, :S], ALU.subtract)
-            nc.scalar.activation(sg[:, t, :], wide[t][:].indirect(n4_t[:]), ACT.Sigmoid, bias=sig_bias[:, col], scale=sl_t[:, col])
+                nc.vector.tensor_tensor(step[t][:], b_n5[:], wide[t][:, :S], ALU.subtract)
+        for t in range(R):
+            col = slice(t, t + 1)
+            nc.scalar.activation(sg[t][:], wide[t][:].indirect(n4_t[:]), ACT.Sigmoid, bias=sig_bias[:, col], scale=sl_t[:, col])
             a_acc = product(w3_q, (z_codes, z_scales), t, R + t)
-            gated = sb([P, S], F32, "gated%d" % t)
-            nc.vector.tensor_tensor(gated[:], a_acc[:], sg[:, t, :], ALU.mult)
-            result = sb([P, S], F32, "result%d" % t)
-            nc.vector.tensor_tensor(result[:], gated[:], step[:], ALU.max)
-            nc.sync.dma_start(out_rows[:, t, :], result[:])
+            if t > 0:
+                finish(t - 1, slice(0, S))
+            if t < R - 1:
+                nc.vector.tensor_tensor(gated[t][:], a_acc[:], sg[t][:], ALU.mult)
+            else:
+                for h in range(2):
+                    cols = slice(h * half, (h + 1) * half)
+                    nc.vector.tensor_tensor(gated[t][:, cols], a_acc[:, cols], sg[t][:, cols], ALU.mult)
+                for h in range(2):
+                    finish(t, slice(h * half, (h + 1) * half))

@@ -16,7 +16,7 @@ P = 128
 R = 4
 S = 512
 T = 2048
-WIDE = 1024
+WIDE = 512
 NARROW = 544
 CHUNK = 128
 FLOPS = 4 * 2 * 512 * 512 * 512
@@ -47,13 +47,10 @@ def tile_picked_tfcdmxbgspanecl_none_p_kernel(
             nc.sync.dma_start(tile[:], src.rearrange("(p t) one -> p (t one)", t=R))
             return tile
 
-        def load_weight(src, name):
-            halves = []
-            for h in range(2):
-                raw = sb([P, R, S // 2], F32, "%s_raw%d" % (name, h))
-                nc.sync.dma_start(raw[:], src[:, h * (S // 2) : (h + 1) * (S // 2)].rearrange("(p j) c -> p j c", j=R))
-                halves.append(raw)
-            return halves
+        def load_half(src, name, h):
+            raw = sb([P, R, S // 2], F32, "%s_raw%d" % (name, h))
+            nc.sync.dma_start(raw[:], src[:, h * (S // 2) : (h + 1) * (S // 2)].rearrange("(p j) c -> p j c", j=R))
+            return raw
 
         def round_weight(halves, name):
             grouped = sb([P, R * S], BF16, name + "_bf16")
@@ -75,8 +72,8 @@ def tile_picked_tfcdmxbgspanecl_none_p_kernel(
             nc.vector.quantize_mx(out=codes[:].bitcast(FP8X4), scales=scales[:], in_=values[:])
             return codes, scales
 
-        def pick(lst, name, deal):
-            codes = sb([P, S], U32, name + "_codes")
+        def pick(lst, name, deal, after):
+            codes = keep.tile([P, S], U32, name=name + "_codes", tag=after, align_bytes=64)
             scales = sb([P, S], U8, name + "_scales")
             for dst, table in ((scales, xs), (codes, xw)):
                 view = dst[:].rearrange("p (t m) -> p m t", t=R) if deal else dst[:]
@@ -103,21 +100,25 @@ def tile_picked_tfcdmxbgspanecl_none_p_kernel(
         xs_landing = sb([P, T], U8, "xs_landing")
         for q in range(4):
             nc.sync.dma_start(xs_landing[32 * q : 32 * q + 4, :].bitcast(I32), x_scales[0, 4 * q : 4 * q + 4, :].bitcast(I32))
+        w1_raw, w2_raw, w3_raw = [None, None], [None, None], [None, None]
         two_t = load_list(two, "two_t")
         offs_t = load_list(offs, "offs_t")
-        nc.sync.dma_start(xw[:].bitcast(I32), x_words[0].rearrange("p n t -> p (n t)").bitcast(I32))
-        w2_raw = load_weight(w2, "w2")
-        tau_t = load_rows(tau, "tau_t")
-        w1_raw = load_weight(w1, "w1")
         cand_t = load_list(cand, "cand_t")
+        w2_raw[0] = load_half(w2, "w2", 0)
+        w2_raw[1] = load_half(w2, "w2", 1)
+        nc.sync.dma_start(xw[:].bitcast(I32), x_words[0].rearrange("p n t -> p (n t)").bitcast(I32))
+        w1_raw[0] = load_half(w1, "w1", 0)
+        tau_t = load_rows(tau, "tau_t")
+        w1_raw[1] = load_half(w1, "w1", 1)
         n2_t = load_list(n2, "n2_t")
+        gn_t = load_rows(gn, "gn_t")
         sl_t = load_rows(sl, "sl_t")
         th_t = load_rows(th, "th_t")
         gs_t = load_rows(gs, "gs_t")
         n3_t = load_list(n3, "n3_t")
         n1_t = load_list(n1, "n1_t")
-        gn_t = load_rows(gn, "gn_t")
-        w3_raw = load_weight(w3, "w3")
+        w3_raw[0] = load_half(w3, "w3", 0)
+        w3_raw[1] = load_half(w3, "w3", 1)
         n4_t = load_list(n4, "n4_t")
         n5_t = load_list(n5, "n5_t")
 
@@ -127,37 +128,40 @@ def tile_picked_tfcdmxbgspanecl_none_p_kernel(
         wide = [sb([P, WIDE], F32, "wide%d" % t) for t in range(R)]
         y_rows = [sb([P, NARROW], F32, "y_rows%d" % t) for t in range(R)]
         half_d = {t: sb([P, NARROW], F32, "half_d%d" % t) for t in N3_FUSED}
-        for t in range(R):
-            nc.vector.memset(wide[t][:, S:], 0.0)
+        halves = [slice(h * S // 2, (h + 1) * S // 2) for h in range(2)]
+
+        def part(lst, cols):
+            return lst[:, cols.start // 16 : cols.stop // 16]
+
         for tile in y_rows + list(half_d.values()):
             nc.vector.memset(tile[:, S:], 0.0)
 
-        x_two = pick(two_t, "x_two", False)
-        x_idx = pick(offs_t, "x_idx", False)
-        neg_tau = sb([P, R], F32, "neg_tau")
-        nc.vector.tensor_scalar(neg_tau[:], tau_t[:], -1.0, None, ALU.mult)
+        x_two = pick(two_t, "x_two", False, "x_two_codes")
         w2_q = quantise(round_weight(w2_raw, "w2"), "w2")
+        x_idx = pick(offs_t, "x_idx", False, "w2_bf16")
         w1_bf16 = round_weight(w1_raw, "w1")
 
-        top = sb([P, R], F32, "top")
-        exp_bias = sb([P, R], F32, "exp_bias")
-        ea = sb([P, R, S], F32, "ea")
+        top = [sb([P, 1], F32, "top%d" % t) for t in range(R)]
+        exp_bias = [sb([P, 1], F32, "exp_bias%d" % t) for t in range(R)]
+        ea = keep.tile([P, R, S], F32, name="ea", tag="w1_raw1", align_bytes=64)
         for t in range(R):
             col = slice(t, t + 1)
             d_acc = product(w2_q, x_two, t, t)
-            nc.vector.tensor_scalar(wide[t][:, :S], d_acc[:], 1.0, None, ALU.mult, ALU.max, accum_out=top[:, col])
-            nc.scalar.activation(exp_bias[:, col], top[:, col], ACT.Copy, scale=neg_tau[:, col])
-            nc.scalar.activation(ea[:, t, :], wide[t][:].indirect(n2_t[:]), ACT.Exp, bias=exp_bias[:, col], scale=tau_t[:, col])
+            nc.vector.tensor_scalar(wide[t][:, :S], d_acc[:], 1.0, None, ALU.mult, ALU.max, accum_out=top[t][:])
+            nc.gpsimd.tensor_scalar(exp_bias[t][:], top[t][:], tau_t[:, col], -1.0, ALU.mult, ALU.mult)
+            for cols in halves:
+                nc.scalar.activation(ea[:, t, cols], wide[t][:].indirect(part(n2_t, cols)), ACT.Exp, bias=exp_bias[t][:], scale=tau_t[:, col])
             if t in N3_FUSED:
-                nc.scalar.activation(half_d[t][:, :S], d_acc[:], ACT.Copy, scale=-0.5)
+                nc.gpsimd.tensor_scalar(half_d[t][:, :S], wide[t][:, :S], -0.5, 0.0, ALU.mult, ALU.add)
         w1_q = quantise(w1_bf16, "w1")
-        x_cand = pick(cand_t, "x_cand", True)
+        x_cand = pick(cand_t, "x_cand", True, "w2_codes")
 
         larger = sb([P, R, S], F32, "larger")
         mixed = sb([P, R, S], F32, "mixed")
         d_n3 = {t: sb([P, S], F32, "d_n3_%d" % t) for t in range(R) if t not in N3_FUSED}
         for t in d_n3:
-            nc.scalar.activation(d_n3[t][:], wide[t][:].indirect(n3_t[:]), ACT.Copy)
+            for cols in halves:
+                nc.scalar.activation(d_n3[t][:, cols], wide[t][:].indirect(part(n3_t, cols)), ACT.Copy)
 
         def finish_mixed(t):
             if t in N3_FUSED:
@@ -244,7 +248,8 @@ def tile_picked_tfcdmxbgspanecl_none_p_kernel(
                     nc.sync.dma_start(b_again[t][:], wide[t][:, :S])
 
         def fused_step(t):
-            nc.vector.tensor_tensor(step[t][:], wide[t][:].indirect(n5_t[:]), b_again[t][:], ALU.subtract)
+            for cols in halves:
+                nc.vector.tensor_tensor(step[t][:, cols], wide[t][:].indirect(part(n5_t, cols)), b_again[t][:, cols], ALU.subtract)
 
         for c in range(chunks + 1):
             if c == 4:
@@ -278,26 +283,25 @@ def tile_picked_tfcdmxbgspanecl_none_p_kernel(
         gated = [sb([P, S], F32, "gated%d" % t) for t in range(R)]
         result = [sb([P, S], F32, "result%d" % t) for t in range(R)]
 
-        def finish(t, cols):
-            nc.vector.tensor_tensor(result[t][:, cols], gated[t][:, cols], step[t][:, cols], ALU.max)
-            nc.sync.dma_start(out_rows[:, t, cols], result[t][:, cols])
-
         for t in range(R):
             if t not in N5_FUSED:
                 b_n5 = sb([P, S], F32, "b_n5_%d" % t)
-                nc.scalar.activation(b_n5[:], wide[t][:].indirect(n5_t[:]), ACT.Copy)
+                for cols in halves:
+                    nc.scalar.activation(b_n5[:, cols], wide[t][:].indirect(part(n5_t, cols)), ACT.Copy)
                 nc.vector.tensor_tensor(step[t][:], b_n5[:], wide[t][:, :S], ALU.subtract)
         for t in range(R):
             col = slice(t, t + 1)
-            nc.scalar.activation(sg[t][:], wide[t][:].indirect(n4_t[:]), ACT.Sigmoid, bias=sig_bias[:, col], scale=sl_t[:, col])
+            for cols in halves:
+                nc.scalar.activation(
+                    sg[t][:, cols], wide[t][:].indirect(n4_t[:, cols.start // 16 : cols.stop // 16]), ACT.Sigmoid, bias=sig_bias[:, col], scale=sl_t[:, col]
+                )
             a_acc = product(w3_q, (z_codes, z_scales), t, R + t)
-            if t > 0:
-                finish(t - 1, slice(0, S))
+            parts = halves if t >= 0 else [slice(0, S)]
+            for cols in parts:
+                nc.vector.tensor_tensor(gated[t][:, cols], a_acc[:, cols], sg[t][:, cols], ALU.mult)
+            for cols in parts:
+                nc.vector.tensor_tensor(result[t][:, cols], gated[t][:, cols], step[t][:, cols], ALU.max)
+                if t == R - 1:
+                    nc.sync.dma_start(out_rows[:, t, cols], result[t][:, cols])
             if t < R - 1:
-                nc.vector.tensor_tensor(gated[t][:], a_acc[:], sg[t][:], ALU.mult)
-            else:
-                for h in range(2):
-                    cols = slice(h * half, (h + 1) * half)
-                    nc.vector.tensor_tensor(gated[t][:, cols], a_acc[:, cols], sg[t][:, cols], ALU.mult)
-                for h in range(2):
-                    finish(t, slice(h * half, (h + 1) * half))
+                nc.sync.dma_start(out_rows[:, t, :], result[t][:])

@@ -55,9 +55,9 @@ def tile_picked_tfcdmxbgspanecl_none_p_kernel(
         def round_weight(halves, name):
             grouped = sb([P, R * S], BF16, name + "_bf16")
             dealt = grouped[:].rearrange("p (t m j) -> p m j t", t=R, j=R)
-            for h, raw in enumerate(halves):
-                dst = dealt[:, h * (P // 2) : (h + 1) * (P // 2)]
-                src = raw[:].rearrange("p j (m t) -> p m j t", t=R)
+            for h, u in ((0, 0), (0, 1), (1, 0), (1, 1)):
+                dst = dealt[:, h * (P // 2) : (h + 1) * (P // 2), :, 2 * u : 2 * u + 2]
+                src = halves[h][:].rearrange("p j (m t) -> p m j t", t=R)[:, :, :, 2 * u : 2 * u + 2]
                 if CAST[name] == "scalar":
                     nc.scalar.copy(dst, src)
                 elif CAST[name] == "vector":
@@ -76,8 +76,12 @@ def tile_picked_tfcdmxbgspanecl_none_p_kernel(
             codes = keep.tile([P, S], U32, name=name + "_codes", tag=after, align_bytes=64)
             scales = sb([P, S], U8, name + "_scales")
             for dst, table in ((scales, xs), (codes, xw)):
-                view = dst[:].rearrange("p (t m) -> p m t", t=R) if deal else dst[:]
-                nc.vector.tensor_copy(view, table[:].indirect(lst[:]))
+                nc.vector.tensor_copy(dst[:], table[:].indirect(lst[:]))
+            if deal:
+                dealt = (sb([P, S], U32, name + "_codes_dealt"), sb([P, S], U8, name + "_scales_dealt"))
+                for dst, src in zip(dealt, (codes, scales)):
+                    nc.vector.tensor_copy(dst[:].rearrange("p (t m) -> p m t", t=R), src[:].rearrange("p (m t) -> p m t", t=R))
+                return dealt
             return codes, scales
 
         def product(stationary, moving, t, bank):
@@ -141,18 +145,20 @@ def tile_picked_tfcdmxbgspanecl_none_p_kernel(
         x_idx = pick(offs_t, "x_idx", False, "w2_bf16")
         w1_bf16 = round_weight(w1_raw, "w1")
 
+        d_banks = []
         top = [sb([P, 1], F32, "top%d" % t) for t in range(R)]
         exp_bias = [sb([P, 1], F32, "exp_bias%d" % t) for t in range(R)]
         ea = keep.tile([P, R, S], F32, name="ea", tag="w1_raw1", align_bytes=64)
         for t in range(R):
             col = slice(t, t + 1)
             d_acc = product(w2_q, x_two, t, t)
+            d_banks.append(d_acc)
             nc.vector.tensor_scalar(wide[t][:, :S], d_acc[:], 1.0, None, ALU.mult, ALU.max, accum_out=top[t][:])
-            nc.gpsimd.tensor_scalar(exp_bias[t][:], top[t][:], tau_t[:, col], -1.0, ALU.mult, ALU.mult)
+            nc.vector.tensor_scalar(exp_bias[t][:], top[t][:], tau_t[:, col], -1.0, ALU.mult, ALU.mult)
             for cols in halves:
                 nc.scalar.activation(ea[:, t, cols], wide[t][:].indirect(part(n2_t, cols)), ACT.Exp, bias=exp_bias[t][:], scale=tau_t[:, col])
             if t in N3_FUSED:
-                nc.gpsimd.tensor_scalar(half_d[t][:, :S], wide[t][:, :S], -0.5, 0.0, ALU.mult, ALU.add)
+                (nc.vector if t in (3,) else nc.gpsimd).tensor_scalar(half_d[t][:, :S], wide[t][:, :S], -0.5, 0.0, ALU.mult, ALU.add)
         w1_q = quantise(w1_bf16, "w1")
         x_cand = pick(cand_t, "x_cand", True, "w2_codes")
 
@@ -170,7 +176,7 @@ def tile_picked_tfcdmxbgspanecl_none_p_kernel(
                 nc.vector.scalar_tensor_tensor(mixed[:, t, :], d_n3[t][:], -0.5, larger[:, t, :], ALU.mult, ALU.add)
 
         for t in range(R):
-            nc.vector.scalar_tensor_tensor(larger[:, t, :], ea[:, t, :], 2.0, wide[t][:, :S], ALU.mult, ALU.max)
+            nc.vector.scalar_tensor_tensor(larger[:, t, :], ea[:, t, :], 2.0, d_banks[t][:], ALU.mult, ALU.max)
             if t > 0:
                 finish_mixed(t - 1)
         finish_mixed(R - 1)
@@ -186,9 +192,9 @@ def tile_picked_tfcdmxbgspanecl_none_p_kernel(
         half = S // 2
         for h in range(2):
             nc.vector.tensor_tensor(
-                z2[:, h * half * R : (h + 1) * half * R].rearrange("p (c i t) -> p c t i", i=4, t=R),
-                mixed[:, :, h * half : (h + 1) * half].rearrange("p t (c i) -> p c t i", i=4),
-                gs_t[:].unsqueeze(1).unsqueeze(3).to_broadcast([P, half // 4, R, 4]),
+                z2[:, h * half * R : (h + 1) * half * R].rearrange("p (c i t) -> p c t i", i=2, t=R),
+                mixed[:, :, h * half : (h + 1) * half].rearrange("p t (c i) -> p c t i", i=2),
+                gs_t[:].unsqueeze(1).unsqueeze(3).to_broadcast([P, half // 2, R, 2]),
                 ALU.mult,
             )
         for h in range(2):
@@ -210,15 +216,15 @@ def tile_picked_tfcdmxbgspanecl_none_p_kernel(
             stage[c, "members"] = members
 
         def pairs(c, op, name):
-            view = stage[c, "members"][:].rearrange("p t (j h e) -> p h j t e", h=2, e=2)
-            tile = ring.tile([P, CHUNK, R, 2], F32, name=name)
-            nc.vector.tensor_tensor(tile[:], view[:, 0], view[:, 1], op)
+            view = stage[c, "members"][:].rearrange("p (u v) (j h e) -> p h j u v e", v=2, h=2, e=2)
+            tile = ring.tile([P, CHUNK, 2, 2, 2], F32, name=name)
+            nc.vector.tensor_tensor(tile[:].rearrange("p j u e v -> p j u v e"), view[:, 0], view[:, 1], op)
             stage[c, name] = tile
 
         def fours(c, op, src, name):
-            view = stage[c, src][:].rearrange("p j t e -> p e (j t)")
+            view = stage[c, src][:].rearrange("p j u e v -> p e (j u) v")
             tile = ring.tile([P, width], F32, name=name)
-            nc.vector.tensor_tensor(tile[:], view[:, 0], view[:, 1], op)
+            nc.vector.tensor_tensor(tile[:].rearrange("p (g v) -> p g v", v=2), view[:, 0], view[:, 1], op)
             stage[c, name] = tile
 
         def spread(c):

from contextlib import ExitStack

import concourse.mybir as mybir

F32 = mybir.dt.float32
BF16 = mybir.dt.bfloat16
I32 = mybir.dt.int32
U32 = mybir.dt.uint32
U16 = mybir.dt.uint16
U8 = mybir.dt.uint8
FP8X4 = mybir.dt.float8_e4m3fn_x4
ALU = mybir.AluOpType
ACT = mybir.ActivationFunctionType

P = 128
R = 4
S = 512
T = 2048
WIDE = 512
NARROW = 544
CHUNK = 128
FLOPS = 4 * 2 * 512 * 512 * 512
N3_FUSED = (0, 1, 2, 3)
N5_FUSED = ()
CAST = {"w1": "scalar", "w2": "scalar", "w3": "vector"}


def tile_picked_tfcdmxbgspanecl_none_p_kernel(
    tc, x_words, x_scales, w1, w2, tau, gn, w3, gs, sl, th, offs, two, n1, n2, n3, cand, n4, n5, out
):
    nc = tc.nc
    with ExitStack() as ctx:
        keep = ctx.enter_context(tc.tile_pool(name="keep", bufs=1))
        ring = ctx.enter_context(tc.tile_pool(name="ring", bufs=2))
        psum = ctx.enter_context(tc.psum_pool(name="psum", bufs=1))

        def sb(shape, dtype, name):
            return keep.tile(shape, dtype, name=name, align_bytes=64)

        def load_list(src, name):
            tile = sb([P, src.shape[1]], U16, name)
            nc.sync.dma_start(tile[:], src)
            return tile

        def load_rows(src, name):
            tile = sb([P, R], F32, name)
            nc.sync.dma_start(tile[:], src.rearrange("(p t) one -> p (t one)", t=R))
            return tile

        def load_half(src, name, h):
            raw = sb([P, R, S // 2], F32, "%s_raw%d" % (name, h))
            nc.sync.dma_start(raw[:], src[:, h * (S // 2) : (h + 1) * (S // 2)].rearrange("(p j) c -> p j c", j=R))
            return raw

        def round_weight(halves, name):
            grouped = sb([P, R * S], BF16, name + "_bf16")
            dealt = grouped[:].rearrange("p (t m j) -> p m j t", t=R, j=R)
            for h, u in ((0, 0), (0, 1), (1, 0), (1, 1)):
                dst = dealt[:, h * (P // 2) : (h + 1) * (P // 2), :, 2 * u : 2 * u + 2]
                src = halves[h][:].rearrange("p j (m t) -> p m j t", t=R)[:, :, :, 2 * u : 2 * u + 2]
                if CAST[name] == "scalar":
                    nc.scalar.copy(dst, src)
                elif CAST[name] == "vector":
                    nc.vector.tensor_copy(dst, src)
                else:
                    nc.gpsimd.tensor_scalar(dst, src, 1.0, 0.0, ALU.mult, ALU.add)
            return grouped

        def quantise(values, name):
            codes = sb([P, S], U32, name + "_codes")
            scales = sb([P, S], U8, name + "_scales")
            nc.vector.quantize_mx(out=codes[:].bitcast(FP8X4), scales=scales[:], in_=values[:])
            return codes, scales

        def pick(lst, name, deal, after):
            codes = keep.tile([P, S], U32, name=name + "_codes", tag=after, align_bytes=64)
            scales = sb([P, S], U8, name + "_scales")
            for dst, table in ((scales, xs), (codes, xw)):
                nc.vector.tensor_copy(dst[:], table[:].indirect(lst[:]))
            if deal:
                dealt = (sb([P, S], U32, name + "_codes_dealt"), sb([P, S], U8, name + "_scales_dealt"))
                for dst, src in zip(dealt, (codes, scales)):
                    nc.vector.tensor_copy(dst[:].rearrange("p (t m) -> p m t", t=R), src[:].rearrange("p (m t) -> p m t", t=R))
                return dealt
            return codes, scales

        def product(stationary, moving, t, bank):
            acc = psum.tile([P, S], F32, name="bank%d" % bank)
            cols = slice(t * P, (t + 1) * P)
            nc.tensor.matmul_mx(
                out=acc[:],
                lhsT=stationary[0][:, cols].bitcast(FP8X4),
                lhsT_scale=stationary[1][:, cols],
                rhs=moving[0][:].bitcast(FP8X4),
                rhs_scale=moving[1][:],
                start=True,
                stop=True,
            )
            return acc

        xw = sb([P, T], U32, "xw")
        xs = sb([P, T], U8, "xs")
        nc.vector.memset(xs[:].bitcast(I32), 0)
        xs_landing = sb([P, T], U8, "xs_landing")
        for q in range(4):
            nc.sync.dma_start(xs_landing[32 * q : 32 * q + 4, :].bitcast(I32), x_scales[0, 4 * q : 4 * q + 4, :].bitcast(I32))
        w1_raw, w2_raw, w3_raw = [None, None], [None, None], [None, None]
        two_t = load_list(two, "two_t")
        offs_t = load_list(offs, "offs_t")
        cand_t = load_list(cand, "cand_t")
        w2_raw[0] = load_half(w2, "w2", 0)
        w2_raw[1] = load_half(w2, "w2", 1)
        nc.sync.dma_start(xw[:].bitcast(I32), x_words[0].rearrange("p n t -> p (n t)").bitcast(I32))
        w1_raw[0] = load_half(w1, "w1", 0)
        tau_t = load_rows(tau, "tau_t")
        w1_raw[1] = load_half(w1, "w1", 1)
        n2_t = load_list(n2, "n2_t")
        gn_t = load_rows(gn, "gn_t")
        sl_t = load_rows(sl, "sl_t")
        th_t = load_rows(th, "th_t")
        gs_t = load_rows(gs, "gs_t")
        n3_t = load_list(n3, "n3_t")
        n1_t = load_list(n1, "n1_t")
        w3_raw[0] = load_half(w3, "w3", 0)
        w3_raw[1] = load_half(w3, "w3", 1)
        n4_t = load_list(n4, "n4_t")
        n5_t = load_list(n5, "n5_t")

        for q in range(4):
            rows = slice(32 * q, 32 * q + 4)
            nc.vector.tensor_copy(xs[rows, :].bitcast(I32), xs_landing[rows, :].bitcast(I32))
        wide = [sb([P, WIDE], F32, "wide%d" % t) for t in range(R)]
        y_rows = [sb([P, NARROW], F32, "y_rows%d" % t) for t in range(R)]
        half_d = {t: sb([P, NARROW], F32, "half_d%d" % t) for t in N3_FUSED}
        halves = [slice(h * S // 2, (h + 1) * S // 2) for h in range(2)]

        def part(lst, cols):
            return lst[:, cols.start // 16 : cols.stop // 16]

        for tile in y_rows + list(half_d.values()):
            nc.vector.memset(tile[:, S:], 0.0)

        x_two = pick(two_t, "x_two", False, "x_two_codes")
        w2_q = quantise(round_weight(w2_raw, "w2"), "w2")
        x_idx = pick(offs_t, "x_idx", False, "w2_bf16")
        w1_bf16 = round_weight(w1_raw, "w1")

        d_banks = []
        top = [sb([P, 1], F32, "top%d" % t) for t in range(R)]
        exp_bias = [sb([P, 1], F32, "exp_bias%d" % t) for t in range(R)]
        ea = keep.tile([P, R, S], F32, name="ea", tag="w1_raw1", align_bytes=64)
        for t in range(R):
            col = slice(t, t + 1)
            d_acc = product(w2_q, x_two, t, t)
            d_banks.append(d_acc)
            nc.vector.tensor_scalar(wide[t][:, :S], d_acc[:], 1.0, None, ALU.mult, ALU.max, accum_out=top[t][:])
            nc.vector.tensor_scalar(exp_bias[t][:], top[t][:], tau_t[:, col], -1.0, ALU.mult, ALU.mult)
            for cols in halves:
                nc.scalar.activation(ea[:, t, cols], wide[t][:].indirect(part(n2_t, cols)), ACT.Exp, bias=exp_bias[t][:], scale=tau_t[:, col])
            if t in N3_FUSED:
                (nc.vector if t in (3,) else nc.gpsimd).tensor_scalar(half_d[t][:, :S], wide[t][:, :S], -0.5, 0.0, ALU.mult, ALU.add)
        w1_q = quantise(w1_bf16, "w1")
        x_cand = pick(cand_t, "x_cand", True, "w2_codes")

        larger = sb([P, R, S], F32, "larger")
        mixed = sb([P, R, S], F32, "mixed")
        d_n3 = {t: sb([P, S], F32, "d_n3_%d" % t) for t in range(R) if t not in N3_FUSED}
        for t in d_n3:
            for cols in halves:
                nc.scalar.activation(d_n3[t][:, cols], wide[t][:].indirect(part(n3_t, cols)), ACT.Copy)

        def finish_mixed(t):
            if t in N3_FUSED:
                nc.vector.tensor_tensor(mixed[:, t, :], half_d[t][:].indirect(n3_t[:]), larger[:, t, :], ALU.add)
            else:
                nc.vector.scalar_tensor_tensor(mixed[:, t, :], d_n3[t][:], -0.5, larger[:, t, :], ALU.mult, ALU.add)

        for t in range(R):
            nc.vector.scalar_tensor_tensor(larger[:, t, :], ea[:, t, :], 2.0, d_banks[t][:], ALU.mult, ALU.max)
            if t > 0:
                finish_mixed(t - 1)
        finish_mixed(R - 1)

        for t in range(R):
            y_acc = product(w1_q, x_idx, t, R + t)
            nc.scalar.copy(y_rows[t][:, :S], y_acc[:])

        sig_bias = sb([P, R], F32, "sig_bias")
        nc.vector.scalar_tensor_tensor(sig_bias[:], sl_t[:], -1.0, th_t[:], ALU.mult, ALU.mult)
        z2 = sb([P, S * R], BF16, "z2")
        z2_q = (sb([P, S], U32, "z2_codes"), sb([P, S], U8, "z2_scales"))
        half = S // 2
        for h in range(2):
            nc.vector.tensor_tensor(
                z2[:, h * half * R : (h + 1) * half * R].rearrange("p (c i t) -> p c t i", i=2, t=R),
                mixed[:, :, h * half : (h + 1) * half].rearrange("p t (c i) -> p c t i", i=2),
                gs_t[:].unsqueeze(1).unsqueeze(3).to_broadcast([P, half // 2, R, 2]),
                ALU.mult,
            )
        for h in range(2):
            cols = slice(h * half, (h + 1) * half)
            nc.vector.quantize_mx(out=z2_q[0][:, cols].bitcast(FP8X4), scales=z2_q[1][:, cols], in_=z2[:, h * half * R : (h + 1) * half * R])
        b_acc = [product(x_cand, z2_q, t, t) for t in range(R)]

        z = sb([P, S * R], BF16, "z")
        z_codes = sb([P, S], U32, "z_codes")
        z_scales = sb([P, S], U8, "z_scales")
        width = CHUNK * R
        chunks = S // CHUNK
        stage = {}

        def fetch(c):
            members = keep.tile([P, R, width], F32, name="members%d" % c)
            for t in range(R):
                nc.scalar.activation(members[:, t, :], y_rows[t][:].indirect(n1_t[:, c * width // 16 : (c + 1) * width // 16]), ACT.Copy)
            stage[c, "members"] = members

        def pairs(c, op, name):
            view = stage[c, "members"][:].rearrange("p (u v) (j h e) -> p h j u v e", v=2, h=2, e=2)
            tile = ring.tile([P, CHUNK, 2, 2, 2], F32, name=name)
            nc.vector.tensor_tensor(tile[:].rearrange("p j u e v -> p j u v e"), view[:, 0], view[:, 1], op)
            stage[c, name] = tile

        def fours(c, op, src, name):
            view = stage[c, src][:].rearrange("p j u e v -> p e (j u) v")
            tile = ring.tile([P, width], F32, name=name)
            nc.vector.tensor_tensor(tile[:].rearrange("p (g v) -> p g v", v=2), view[:, 0], view[:, 1], op)
            stage[c, name] = tile

        def spread(c):
            tile = ring.tile([P, width], F32, name="spread")
            nc.vector.scalar_tensor_tensor(tile[:], stage[c, "mn"][:], -0.5, stage[c, "mx"][:], ALU.mult, ALU.add)
            stage[c, "spread"] = tile

        def gain(c):
            nc.vector.tensor_tensor(
                z[:, c * width : (c + 1) * width].rearrange("p (j t) -> p j t", t=R),
                stage[c, "spread"][:].rearrange("p (j t) -> p j t", t=R),
                gn_t[:].unsqueeze(1).to_broadcast([P, CHUNK, R]),
                ALU.mult,
            )

        def quantise_chunk(c):
            cols = slice(c * CHUNK, (c + 1) * CHUNK)
            nc.vector.quantize_mx(out=z_codes[:, cols].bitcast(FP8X4), scales=z_scales[:, cols], in_=z[:, c * width : (c + 1) * width])

        b_again = {t: sb([P, S], F32, "b_again%d" % t) for t in N5_FUSED}
        step = [sb([P, S], F32, "step%d" % t) for t in range(R)]

        def empty_b():
            for t in range(R):
                nc.scalar.activation(wide[t][:, :S], b_acc[t][:], ACT.Copy, scale=0.0625)
                if t in N5_FUSED:
                    nc.sync.dma_start(b_again[t][:], wide[t][:, :S])

        def fused_step(t):
            for cols in halves:
                nc.vector.tensor_tensor(step[t][:, cols], wide[t][:].indirect(part(n5_t, cols)), b_again[t][:, cols], ALU.subtract)

        for c in range(chunks + 1):
            if c == 4:
                empty_b()
            if c == 0:
                w3_bf16 = round_weight(w3_raw, "w3")
            if c == 4:
                for t in N5_FUSED:
                    fused_step(t)
            if c < chunks:
                fetch(c)
                pairs(c, ALU.max, "hi")
            if c > 0:
                spread(c - 1)
            if c < chunks:
                pairs(c, ALU.min, "lo")
            if c > 0:
                gain(c - 1)
            if c < chunks:
                fours(c, ALU.max, "hi", "mx")
            if c == chunks:
                w3_q = quantise(w3_bf16, "w3")
            if c > 0:
                quantise_chunk(c - 1)
            if c < chunks:
                fours(c, ALU.min, "lo", "mn")


        out_rows = out.rearrange("(p t) n -> p t n", t=R)
        sg = [sb([P, S], F32, "sg%d" % t) for t in range(R)]
        gated = [sb([P, S], F32, "gated%d" % t) for t in range(R)]
        result = [sb([P, S], F32, "result%d" % t) for t in range(R)]

        for t in range(R):
            if t not in N5_FUSED:
                b_n5 = sb([P, S], F32, "b_n5_%d" % t)
                for cols in halves:
                    nc.scalar.activation(b_n5[:, cols], wide[t][:].indirect(part(n5_t, cols)), ACT.Copy)
                nc.vector.tensor_tensor(step[t][:], b_n5[:], wide[t][:, :S], ALU.subtract)
        for t in range(R):
            col = slice(t, t + 1)
            for cols in halves:
                nc.scalar.activation(
                    sg[t][:, cols], wide[t][:].indirect(n4_t[:, cols.start // 16 : cols.stop // 16]), ACT.Sigmoid, bias=sig_bias[:, col], scale=sl_t[:, col]
                )
            a_acc = product(w3_q, (z_codes, z_scales), t, R + t)
            parts = halves if t >= 0 else [slice(0, S)]
            for cols in parts:
                nc.vector.tensor_tensor(gated[t][:, cols], a_acc[:, cols], sg[t][:, cols], ALU.mult)
            for cols in parts:
                nc.vector.tensor_tensor(result[t][:, cols], gated[t][:, cols], step[t][:, cols], ALU.max)
                if t == R - 1:
                    nc.sync.dma_start(out_rows[:, t, cols], result[t][:, cols])
            if t < R - 1:
                nc.sync.dma_start(out_rows[:, t, :], result[t][:])
